import numpy as np
import ml_dtypes


def mxq(x, axis, fmt="e4m3"):
    dtype, down = {"e4m3": (ml_dtypes.float8_e4m3fn, 7), "e5m2": (ml_dtypes.float8_e5m2, 14)}[fmt]
    v = np.moveaxis(np.asarray(x, np.float32).astype(ml_dtypes.bfloat16).astype(np.float64), axis, -1)
    blocks = v.reshape(v.shape[:-1] + (-1, 32))
    amax = np.abs(blocks).max(-1, keepdims=True)
    byte = np.maximum(np.where(amax > 0, np.frexp(amax)[1] - 1 + 127, 0) - down, 1)
    scale = np.exp2(byte - 127.0)
    codes = (blocks / scale).astype(np.float32).astype(dtype).astype(np.float64)
    return np.moveaxis((codes * scale).reshape(v.shape), -1, axis)


WIDE = False


def mx_kscale(k):
    if not WIDE:
        return np.ones(k)
    levels = np.array([10, -10, 5, -5, 0])
    if k % 512:
        return np.exp2(np.random.permutation(np.resize(levels, k // 32))).repeat(32)
    a = np.empty((k // 512, 16))
    for p in range(k // 512):
        a[p, :8] = np.random.permutation(np.resize(levels, 8))
        for g in range(8):
            far = levels[np.abs(levels - a[p, g]) >= 10]
            a[p, g + 8] = far[np.random.randint(len(far))]
    return np.exp2(a.ravel()).repeat(32)


def f64(x):
    return np.asarray(x).astype(np.float64)


def striped(idx):
    return np.tile(idx.reshape(-1, 16).T, (8, 1)).astype(np.uint16)


def unstriped(offs):
    return offs[:16].T.reshape(-1).astype(np.int64)


def striped8(idx):
    return np.concatenate([x.reshape(-1, 16).T for x in idx]).astype(np.uint16)


def runs(offs, k):
    lists = np.stack([offs[16 * r : 16 * r + 16].T.reshape(-1) for r in range(8)]).astype(np.int64)
    return lists[np.arange(k) % 512 // 64]


def pack_weight(w):
    k, n = w.shape
    w = f64(np.asarray(w, np.float32).astype(ml_dtypes.bfloat16)).reshape(k // 32, 32, n)
    amax = np.abs(w).max(1)
    byte = np.clip(np.where(amax > 0, np.frexp(amax)[1] - 1 + 127 - 7, 1), 1, 254)
    scaled = (w * np.exp2(127.0 - byte)[:, None, :]).reshape(k, n).astype(np.float32)
    words = np.ascontiguousarray(scaled.reshape(k // 512, 128, 4, n).transpose(0, 1, 3, 2)).astype(ml_dtypes.float8_e4m3fn).view(np.uint8)
    return words, np.ascontiguousarray(byte.astype(np.uint8).reshape(k // 512, 16, n))


def unpack_weight(words, scales):
    g, p, n, _ = words.shape
    vals = np.ascontiguousarray(words).view(ml_dtypes.float8_e4m3fn).astype(np.float64) * np.repeat(np.exp2(scales.astype(np.float64) - 127.0), 8, axis=1)[..., None]
    return vals.transpose(0, 1, 3, 2).reshape(g * 512, n)

def planes(y):
    n, m = y.shape
    v = y.astype(np.float32).astype(ml_dtypes.bfloat16).astype(np.float64).reshape(n // 32, 32, m)
    top = np.abs(v).max(1)
    byte = np.clip(np.where(top > 0, np.frexp(top)[1] - 1 + 127 - 7, 1), 1, 254)
    codes = (v * np.exp2(127.0 - byte)[:, None, :]).reshape(n, m).astype(np.float32).astype(ml_dtypes.float8_e4m3fn).view(np.uint8)
    words = codes.reshape(n // 512, 128, 4, m).transpose(0, 1, 3, 2)
    return np.ascontiguousarray(words), np.ascontiguousarray(byte.astype(np.uint8).reshape(n // 512, 16, m))


K, T, S, G, H, W = 512, 1024, 512, 2048, 512, 256


def setup_inputs():
    n = np.random.standard_normal
    s = mx_kscale(K)[:, None]
    packed_xT = pack_weight(n((K, T)) * s)
    packed_dT = pack_weight(n((K, G)) / s)
    perm = np.stack([np.random.permutation(S) for _ in range(8)])
    return {
        "x_words": packed_xT[0],
        "x_scales": packed_xT[1],
        "d_words": packed_dT[0],
        "d_scales": packed_dT[1],
        "gs": (np.random.uniform(0.5, 1.5, (K, 1)) * s).astype(np.float32),
        "offs": striped(np.random.permutation(T)[:S]),
        "k1": striped8(np.random.randint(0, G, (8, H))),
        "n1": striped8(perm[:, :W]),
        "n2": striped8(perm[:, W:]),
        "k2": striped8(np.random.randint(0, G, (8, H))),
        "n3": striped8(np.stack([np.random.permutation(S) for _ in range(8)])),
        "n4": striped8(np.stack([np.random.permutation(S) for _ in range(8)])),
    }


def reference(x_words, x_scales, d_words, d_scales, gs, offs, k1, n1, n2, k2, n3, n4):
    d_k2 = unpack_weight(d_words, d_scales)[np.arange(K)[:, None], runs(k2, K)]
    d_k1 = unpack_weight(d_words, d_scales)[np.arange(K)[:, None], runs(k1, K)]
    xq = unpack_weight(x_words, x_scales)[:, unstriped(offs)]
    h = 0.0625 * (d_k1.T @ xq)
    pa = h[np.arange(H)[:, None], runs(n1, H)]
    pb = h[np.arange(H)[:, None], runs(n2, H)]
    ra = np.maximum(pa, pb)
    ds = h.copy()
    ds[np.arange(H)[:, None], runs(n1, H)] = ra
    z = f64(gs) * ds
    h2 = 0.0625 * ((d_k2.T @ mxq(z, 0, "e4m3")))
    st = np.maximum(h2, h2[np.arange(H)[:, None], runs(n3, H)])
    out_0 = np.minimum(st, st[np.arange(H)[:, None], runs(n4, H)])
    return (out_0,) + planes(out_0)

@@ -1,0 +1,223 @@
+from contextlib import ExitStack
+
+import concourse.mybir as mybir
+
+K, T, S, G, H, W = 512, 1024, 512, 2048, 512, 256
+FLOPS = 2 * 2 * K * H * S
+
+F32 = mybir.dt.float32
+BF16 = mybir.dt.bfloat16
+I32 = mybir.dt.int32
+U32 = mybir.dt.uint32
+U16 = mybir.dt.uint16
+U8 = mybir.dt.uint8
+FP8X4 = mybir.dt.float8_e4m3fn_x4
+COPY = mybir.ActivationFunctionType.Copy
+ALU = mybir.AluOpType
+
+P = 128
+PACK = 4
+SIXTEENTH = 0.0625
+HALF = S // 2
+Z_SPLIT = 320
+OUT_CHUNKS = ((0, 256), (256, 128), (384, 128))
+
+
+def tile_picked_codefillhopmn_none_po_kernel(
+    tc, x_words, x_scales, d_words, d_scales, gs, offs, k1, n1, n2, k2, n3, n4, out_0, out_1, out_2
+):
+    nc = tc.nc
+
+    with ExitStack() as ctx:
+        lists = ctx.enter_context(tc.tile_pool(name="lists", bufs=1))
+        sb = ctx.enter_context(tc.tile_pool(name="sb", bufs=1))
+        psum = ctx.enter_context(tc.psum_pool(name="psum", bufs=1))
+
+        def sbuf(name, width, dtype):
+            return sb.tile([P] + list(width), dtype, name=name, align_bytes=64)
+
+        def load_list(name, src):
+            held = lists.tile(list(src.shape), U16, name=name)
+            nc.sync.dma_start(held[:], src)
+            return held
+
+        def entries(held, first, count):
+            return held[:, first // 16 : (first + count) // 16]
+
+        def zero_bytes(t):
+            nc.vector.memset(t[:].bitcast(I32), 0)
+
+        def gather_f32(on_vector, out, window, offsets):
+            if on_vector:
+                nc.vector.tensor_copy(out, window[:].indirect(offsets))
+            else:
+                nc.scalar.activation(out, window[:].indirect(offsets), COPY)
+
+        def deal_words(dst, src):
+            nc.vector.tensor_copy(
+                dst.rearrange("p (t c i) -> p c t i", t=PACK, i=4),
+                src.rearrange("p (c i t) -> p c t i", t=PACK, i=4),
+            )
+
+        def deal_bytes(dst, src):
+            nc.vector.tensor_copy(
+                dst.rearrange("p (t m) -> p t m", t=PACK),
+                src.rearrange("p (m t) -> p t m", t=PACK),
+            )
+
+        def place_scale_rows(dst, src):
+            for j in range(4):
+                nc.sync.dma_start(dst[:].bitcast(I32)[j:P:32, :], src[:].bitcast(I32)[8 * j : P : 32, :])
+
+        def interleave(engine_copy, dst, src):
+            engine_copy(
+                dst.rearrange("p (c i) t -> p c t i", i=4),
+                src.rearrange("p t (c i) -> p c t i", i=4),
+            )
+
+        x_table_bytes = sbuf("x_table_bytes", [T], U8)
+        d_table_bytes = sbuf("d_table_bytes", [G], U8)
+        zero_bytes(x_table_bytes)
+        zero_bytes(d_table_bytes)
+        offs_l = load_list("offs_l", offs)
+        k1_l = load_list("k1_l", k1)
+        n1_l = load_list("n1_l", n1)
+        n2_l = load_list("n2_l", n2)
+        nc.sync.dma_start(x_table_bytes[:].bitcast(I32)[0:P:8, :], x_scales[0].bitcast(I32))
+        nc.sync.dma_start(d_table_bytes[:].bitcast(I32)[0:P:8, :], d_scales[0].bitcast(I32))
+        x_table_words = sbuf("x_table_words", [T], U32)
+        d_table_words = sbuf("d_table_words", [G], U32)
+        nc.sync.dma_start(x_table_words[:].bitcast(I32), x_words[0].rearrange("p n t -> p (n t)").bitcast(I32))
+        nc.sync.dma_start(d_table_words[:].bitcast(I32), d_words[0].rearrange("p n t -> p (n t)").bitcast(I32))
+        k2_l = load_list("k2_l", k2)
+        gs_t = sbuf("gs_t", [PACK], F32)
+        nc.gpsimd.dma_start(gs_t[:], gs.rearrange("(p t) o -> p (t o)", t=PACK))
+        n3_l = load_list("n3_l", n3)
+        n4_l = load_list("n4_l", n4)
+
+        scales1 = sbuf("scales1", [S + H], U8)
+        scales2 = sbuf("scales2", [H], U8)
+        zero_bytes(scales1)
+        zero_bytes(scales2)
+
+        picked_bytes1 = sbuf("picked_bytes1", [S + H], U8)
+        dealt_bytes1 = sbuf("dealt_bytes1", [S + H], U8)
+        nc.vector.tensor_copy(picked_bytes1[:, :S], x_table_bytes[:].indirect(offs_l[:]))
+        nc.vector.tensor_copy(picked_bytes1[:, S:], d_table_bytes[:].indirect(k1_l[:]))
+        nc.vector.tensor_copy(dealt_bytes1[:].bitcast(I32)[:, : S // 4], picked_bytes1[:].bitcast(I32)[:, : S // 4])
+        deal_bytes(dealt_bytes1[:, S:], picked_bytes1[:, S:])
+        place_scale_rows(scales1, dealt_bytes1)
+
+        x_picked = sbuf("x_picked", [S], U32)
+        w1_picked = sbuf("w1_picked", [H], U32)
+        w1 = sbuf("w1", [H], U32)
+        nc.vector.tensor_copy(x_picked[:], x_table_words[:].indirect(offs_l[:]))
+        nc.vector.tensor_copy(w1_picked[:], d_table_words[:].indirect(k1_l[:]))
+        deal_words(w1[:], w1_picked[:])
+
+        banks1 = [psum.tile([P, S], F32, name=f"bank1_{t}") for t in range(PACK)]
+        for t in range(PACK):
+            nc.tensor.matmul_mx(
+                out=banks1[t][:],
+                lhsT=w1[:, t * P : (t + 1) * P].bitcast(FP8X4),
+                lhsT_scale=scales1[:, S + t * P : S + (t + 1) * P],
+                rhs=x_picked[:].bitcast(FP8X4),
+                rhs_scale=scales1[:, :S],
+                start=True,
+                stop=True,
+            )
+
+        picked_bytes2 = sbuf("picked_bytes2", [H], U8)
+        dealt_bytes2 = sbuf("dealt_bytes2", [H], U8)
+        nc.vector.tensor_copy(picked_bytes2[:], d_table_bytes[:].indirect(k2_l[:]))
+        deal_bytes(dealt_bytes2[:], picked_bytes2[:])
+        place_scale_rows(scales2, dealt_bytes2)
+        w2_picked = sbuf("w2_picked", [H], U32)
+        w2 = sbuf("w2", [H], U32)
+        nc.vector.tensor_copy(w2_picked[:], d_table_words[:].indirect(k2_l[:]))
+        deal_words(w2[:], w2_picked[:])
+
+        ds = [sbuf(f"ds{t}", [S], F32) for t in range(PACK)]
+        for group in ((0,), (1,), (2, 3)):
+            pa = sbuf(f"pa{group[0]}", [len(group) * W], F32)
+            pb = sbuf(f"pb{group[0]}", [len(group) * W], F32)
+            ra = sbuf(f"ra{group[0]}", [len(group) * W], F32)
+            for u, t in enumerate(group):
+                nc.scalar.activation(ds[t][:], banks1[t][:], COPY, scale=SIXTEENTH)
+                gather_f32(False, pa[:, u * W : (u + 1) * W], ds[t], n1_l[:])
+                gather_f32(False, pb[:, u * W : (u + 1) * W], ds[t], n2_l[:])
+            nc.vector.tensor_tensor(ra[:], pa[:], pb[:], ALU.max)
+            for u, t in enumerate(group):
+                nc.vector.tensor_copy(ds[t][:].indirect(n1_l[:]), ra[:, u * W : (u + 1) * W])
+
+        z_rows = sbuf("z_rows", [PACK, S], BF16)
+        z_grouped = sbuf("z_grouped", [S, PACK], BF16)
+        z_words = sbuf("z_words", [S], U32)
+        z_scales = sbuf("z_scales", [S], U8)
+        last = PACK - 1
+        split = Z_SPLIT
+        for t in range(last):
+            nc.scalar.activation(z_rows[:, t, :], ds[t][:], COPY, scale=gs_t[:, t : t + 1])
+        nc.scalar.activation(z_rows[:, last, split:], ds[last][:, split:], COPY, scale=gs_t[:, last : last + 1])
+        interleave(nc.scalar.copy, z_grouped[:, split:, :], z_rows[:, :, split:])
+        vector_cols = (slice(0, HALF), slice(HALF, split))
+        for cols in vector_cols:
+            nc.vector.tensor_scalar(z_rows[:, last, cols], ds[last][:, cols], gs_t[:, last : last + 1], None, ALU.mult)
+        for cols in vector_cols:
+            interleave(nc.vector.tensor_copy, z_grouped[:, cols, :], z_rows[:, :, cols])
+        for c in range(2):
+            cols = slice(c * HALF, (c + 1) * HALF)
+            nc.vector.quantize_mx(
+                out=z_words[:, cols].bitcast(FP8X4),
+                scales=z_scales[:, cols],
+                in_=z_grouped[:, cols, :].rearrange("p j t -> p (j t)"),
+            )
+
+        banks2 = [psum.tile([P, S], F32, name=f"bank2_{t}") for t in range(PACK)]
+        for t in range(PACK):
+            for c in range(2):
+                cols = slice(c * HALF, (c + 1) * HALF)
+                nc.tensor.matmul_mx(
+                    out=banks2[t][:, cols],
+                    lhsT=w2[:, t * P : (t + 1) * P].bitcast(FP8X4),
+                    lhsT_scale=scales2[:, t * P : (t + 1) * P],
+                    rhs=z_words[:, cols].bitcast(FP8X4),
+                    rhs_scale=z_scales[:, cols],
+                    start=True,
+                    stop=True,
+                )
+
+        h2 = [sbuf(f"h2_{t}", [S], F32) for t in range(PACK)]
+        hop3 = [sbuf(f"hop3_{t}", [S], F32) for t in range(PACK)]
+        st = [sbuf(f"st{t}", [S], F32) for t in range(PACK)]
+        for t in range(PACK):
+            nc.scalar.activation(h2[t][:], banks2[t][:], COPY, scale=SIXTEENTH)
+        for half in range(2 * PACK):
+            t, first = half // 2, half % 2 * HALF
+            gather_f32(half < 3, hop3[t][:, first : first + HALF], h2[t], entries(n3_l, first, HALF))
+        for t in range(PACK):
+            nc.vector.tensor_tensor(st[t][:], h2[t][:], hop3[t][:], ALU.max)
+
+        out_rows = out_0.rearrange("(p t) j -> p t j", t=PACK)
+        out_words = out_1[0].rearrange("p n t -> p (n t)").bitcast(I32)
+        y_scales = sbuf("y_scales", [S], U8)
+        for c, (first, width) in enumerate(OUT_CHUNKS):
+            cols = slice(first, first + width)
+            y = sbuf(f"y{c}", [PACK, width], F32)
+            for t in range(PACK):
+                hop4 = sbuf(f"hop4_{c}_{t}", [width], F32)
+                gather_f32(c == 0 and t < 1, hop4[:], st[t], entries(n4_l, first, width))
+                nc.vector.tensor_tensor(y[:, t, :], st[t][:, cols], hop4[:], ALU.min)
+            nc.sync.dma_start(out_rows[:, :, cols], y[:])
+            y_grouped = sbuf(f"y_grouped{c}", [width, PACK], BF16)
+            y_words = sbuf(f"y_words{c}", [width], U32)
+            interleave(nc.vector.tensor_copy, y_grouped[:], y[:])
+            nc.vector.quantize_mx(
+                out=y_words[:].bitcast(FP8X4),
+                scales=y_scales[:, cols],
+                in_=y_grouped[:].rearrange("p j t -> p (j t)"),
+            )
+            nc.sync.dma_start(out_words[:, cols], y_words[:].bitcast(I32))
+        for q in range(4):
+            queue = nc.sync if q % 2 == 0 else nc.scalar
+            queue.dma_start(out_2[0].bitcast(I32)[4 * q : 4 * q + 4, :], y_scales[:].bitcast(I32)[32 * q : 32 * q + 4, :])

@@ -20,7 +20,8 @@ PACK = 4
 SIXTEENTH = 0.0625
 HALF = S // 2
 Z_SPLIT = 320
-OUT_CHUNKS = ((0, 256), (256, 128), (384, 128))
+QUARTER = S // 4
+N3_HALVES_ON_VECTOR = 4
 
 
 def tile_picked_codefillhopmn_none_po_kernel(
@@ -33,8 +34,8 @@ def tile_picked_codefillhopmn_none_po_kernel(
         sb = ctx.enter_context(tc.tile_pool(name="sb", bufs=1))
         psum = ctx.enter_context(tc.psum_pool(name="psum", bufs=1))
 
-        def sbuf(name, width, dtype):
-            return sb.tile([P] + list(width), dtype, name=name, align_bytes=64)
+        def sbuf(name, width, dtype, tag=""):
+            return sb.tile([P] + list(width), dtype, name=name, tag=tag or name, align_bytes=64)
 
         def load_list(name, src):
             held = lists.tile(list(src.shape), U16, name=name)
@@ -55,7 +56,7 @@ def tile_picked_codefillhopmn_none_po_kernel(
 
         def deal_words(dst, src):
             nc.vector.tensor_copy(
-                dst.rearrange("p (t c i) -> p c t i", t=PACK, i=4),
+                dst.rearrange("p t (c i) -> p c t i", i=4),
                 src.rearrange("p (c i t) -> p c t i", t=PACK, i=4),
             )
 
@@ -65,9 +66,9 @@ def tile_picked_codefillhopmn_none_po_kernel(
                 src.rearrange("p (m t) -> p t m", t=PACK),
             )
 
-        def place_scale_rows(dst, src):
+        def place_scale_rows(dst, src, queues):
             for j in range(4):
-                nc.sync.dma_start(dst[:].bitcast(I32)[j:P:32, :], src[:].bitcast(I32)[8 * j : P : 32, :])
+                queues[j % len(queues)].dma_start(dst[:].bitcast(I32)[j:P:32, :], src[:].bitcast(I32)[8 * j : P : 32, :])
 
         def interleave(engine_copy, dst, src):
             engine_copy(
@@ -77,21 +78,21 @@ def tile_picked_codefillhopmn_none_po_kernel(
 
         x_table_bytes = sbuf("x_table_bytes", [T], U8)
         d_table_bytes = sbuf("d_table_bytes", [G], U8)
-        zero_bytes(x_table_bytes)
         zero_bytes(d_table_bytes)
-        offs_l = load_list("offs_l", offs)
+        zero_bytes(x_table_bytes)
         k1_l = load_list("k1_l", k1)
+        offs_l = load_list("offs_l", offs)
         n1_l = load_list("n1_l", n1)
         n2_l = load_list("n2_l", n2)
-        nc.sync.dma_start(x_table_bytes[:].bitcast(I32)[0:P:8, :], x_scales[0].bitcast(I32))
         nc.sync.dma_start(d_table_bytes[:].bitcast(I32)[0:P:8, :], d_scales[0].bitcast(I32))
+        nc.sync.dma_start(x_table_bytes[:].bitcast(I32)[0:P:8, :], x_scales[0].bitcast(I32))
         x_table_words = sbuf("x_table_words", [T], U32)
         d_table_words = sbuf("d_table_words", [G], U32)
         nc.sync.dma_start(x_table_words[:].bitcast(I32), x_words[0].rearrange("p n t -> p (n t)").bitcast(I32))
         nc.sync.dma_start(d_table_words[:].bitcast(I32), d_words[0].rearrange("p n t -> p (n t)").bitcast(I32))
         k2_l = load_list("k2_l", k2)
         gs_t = sbuf("gs_t", [PACK], F32)
-        nc.gpsimd.dma_start(gs_t[:], gs.rearrange("(p t) o -> p (t o)", t=PACK))
+        nc.sync.dma_start(gs_t[:], gs.rearrange("(p t) o -> p (t o)", t=PACK))
         n3_l = load_list("n3_l", n3)
         n4_l = load_list("n4_l", n4)
 
@@ -102,24 +103,26 @@ def tile_picked_codefillhopmn_none_po_kernel(
 
         picked_bytes1 = sbuf("picked_bytes1", [S + H], U8)
         dealt_bytes1 = sbuf("dealt_bytes1", [S + H], U8)
-        nc.vector.tensor_copy(picked_bytes1[:, :S], x_table_bytes[:].indirect(offs_l[:]))
         nc.vector.tensor_copy(picked_bytes1[:, S:], d_table_bytes[:].indirect(k1_l[:]))
-        nc.vector.tensor_copy(dealt_bytes1[:].bitcast(I32)[:, : S // 4], picked_bytes1[:].bitcast(I32)[:, : S // 4])
+        nc.vector.tensor_copy(picked_bytes1[:, :S], x_table_bytes[:].indirect(offs_l[:]))
         deal_bytes(dealt_bytes1[:, S:], picked_bytes1[:, S:])
-        place_scale_rows(scales1, dealt_bytes1)
+        nc.vector.tensor_copy(dealt_bytes1[:].bitcast(I32)[:, : S // 4], picked_bytes1[:].bitcast(I32)[:, : S // 4])
+        place_scale_rows(scales1, dealt_bytes1, (nc.sync,))
 
         x_picked = sbuf("x_picked", [S], U32)
-        w1_picked = sbuf("w1_picked", [H], U32)
-        w1 = sbuf("w1", [H], U32)
+        w1 = sbuf("w1", [PACK, P], U32)
         nc.vector.tensor_copy(x_picked[:], x_table_words[:].indirect(offs_l[:]))
-        nc.vector.tensor_copy(w1_picked[:], d_table_words[:].indirect(k1_l[:]))
-        deal_words(w1[:], w1_picked[:])
+        w1_picked = [sbuf(f"w1_picked{u}", [H // 2], U32, tag=f"picked{u}") for u in range(2)]
+        for u in range(2):
+            nc.vector.tensor_copy(w1_picked[u][:], d_table_words[:].indirect(entries(k1_l, u * H // 2, H // 2)))
+        for u in range(2):
+            deal_words(w1[:, :, u * P // 2 : (u + 1) * P // 2], w1_picked[u][:])
 
-        banks1 = [psum.tile([P, S], F32, name=f"bank1_{t}") for t in range(PACK)]
+        banks1 = [psum.tile([P, S], F32, name=f"bank1_{t}", tag=f"bank{t}") for t in range(PACK)]
         for t in range(PACK):
             nc.tensor.matmul_mx(
                 out=banks1[t][:],
-                lhsT=w1[:, t * P : (t + 1) * P].bitcast(FP8X4),
+                lhsT=w1[:, t, :].bitcast(FP8X4),
                 lhsT_scale=scales1[:, S + t * P : S + (t + 1) * P],
                 rhs=x_picked[:].bitcast(FP8X4),
                 rhs_scale=scales1[:, :S],
@@ -127,18 +130,18 @@ def tile_picked_codefillhopmn_none_po_kernel(
                 stop=True,
             )
 
-        picked_bytes2 = sbuf("picked_bytes2", [H], U8)
+        w2_picked = sbuf("w2_picked", [H], U32, tag="picked0")
+        picked_bytes2 = sbuf("picked_bytes2", [H], U8, tag="picked1")
         dealt_bytes2 = sbuf("dealt_bytes2", [H], U8)
-        nc.vector.tensor_copy(picked_bytes2[:], d_table_bytes[:].indirect(k2_l[:]))
-        deal_bytes(dealt_bytes2[:], picked_bytes2[:])
-        place_scale_rows(scales2, dealt_bytes2)
-        w2_picked = sbuf("w2_picked", [H], U32)
-        w2 = sbuf("w2", [H], U32)
+        w2 = sbuf("w2", [PACK, P], U32)
         nc.vector.tensor_copy(w2_picked[:], d_table_words[:].indirect(k2_l[:]))
+        nc.vector.tensor_copy(picked_bytes2[:], d_table_bytes[:].indirect(k2_l[:]))
         deal_words(w2[:], w2_picked[:])
+        deal_bytes(dealt_bytes2[:], picked_bytes2[:])
+        place_scale_rows(scales2, dealt_bytes2, (nc.sync,))
 
         ds = [sbuf(f"ds{t}", [S], F32) for t in range(PACK)]
-        for group in ((0,), (1,), (2, 3)):
+        for group in ((0,), (1,), (2,), (3,)):
             pa = sbuf(f"pa{group[0]}", [len(group) * W], F32)
             pb = sbuf(f"pb{group[0]}", [len(group) * W], F32)
             ra = sbuf(f"ra{group[0]}", [len(group) * W], F32)
@@ -173,51 +176,75 @@ def tile_picked_codefillhopmn_none_po_kernel(
                 in_=z_grouped[:, cols, :].rearrange("p j t -> p (j t)"),
             )
 
-        banks2 = [psum.tile([P, S], F32, name=f"bank2_{t}") for t in range(PACK)]
-        for t in range(PACK):
-            for c in range(2):
-                cols = slice(c * HALF, (c + 1) * HALF)
-                nc.tensor.matmul_mx(
-                    out=banks2[t][:, cols],
-                    lhsT=w2[:, t * P : (t + 1) * P].bitcast(FP8X4),
-                    lhsT_scale=scales2[:, t * P : (t + 1) * P],
-                    rhs=z_words[:, cols].bitcast(FP8X4),
-                    rhs_scale=z_scales[:, cols],
-                    start=True,
-                    stop=True,
-                )
-
+        halves = (slice(0, HALF), slice(HALF, S))
         h2 = [sbuf(f"h2_{t}", [S], F32) for t in range(PACK)]
+        pieces = [(0, halves[0]), (0, halves[1])] + [(t, slice(0, S)) for t in range(1, PACK)]
+        for u, (t, cols) in enumerate(pieces):
+            bank = psum.tile([P, S], F32, name=f"bank2_{u}", tag=f"bank{(PACK + u) % 8}")
+            nc.tensor.matmul_mx(
+                out=bank[:, cols],
+                lhsT=w2[:, t, :].bitcast(FP8X4),
+                lhsT_scale=scales2[:, t * P : (t + 1) * P],
+                rhs=z_words[:, cols].bitcast(FP8X4),
+                rhs_scale=z_scales[:, cols],
+                start=True,
+                stop=True,
+            )
+            nc.scalar.activation(h2[t][:, cols], bank[:, cols], COPY, scale=SIXTEENTH)
+
         hop3 = [sbuf(f"hop3_{t}", [S], F32) for t in range(PACK)]
         st = [sbuf(f"st{t}", [S], F32) for t in range(PACK)]
-        for t in range(PACK):
-            nc.scalar.activation(h2[t][:], banks2[t][:], COPY, scale=SIXTEENTH)
-        for half in range(2 * PACK):
-            t, first = half // 2, half % 2 * HALF
-            gather_f32(half < 3, hop3[t][:, first : first + HALF], h2[t], entries(n3_l, first, HALF))
-        for t in range(PACK):
-            nc.vector.tensor_tensor(st[t][:], h2[t][:], hop3[t][:], ALU.max)
-
+        hop4 = [[sbuf(f"hop4_{c}_{t}", [HALF], F32) for t in range(PACK)] for c in range(2)]
+        y = [sbuf(f"y{c}", [PACK, HALF], F32) for c in range(2)]
+        y_grouped = [sbuf(f"y_grouped{c}", [HALF, PACK], BF16) for c in range(2)]
+        y_words = [sbuf(f"y_words{c}", [HALF], U32) for c in range(2)]
+        y_scales = sbuf("y_scales", [S], U8)
         out_rows = out_0.rearrange("(p t) j -> p t j", t=PACK)
         out_words = out_1[0].rearrange("p n t -> p (n t)").bitcast(I32)
-        y_scales = sbuf("y_scales", [S], U8)
-        for c, (first, width) in enumerate(OUT_CHUNKS):
-            cols = slice(first, first + width)
-            y = sbuf(f"y{c}", [PACK, width], F32)
-            for t in range(PACK):
-                hop4 = sbuf(f"hop4_{c}_{t}", [width], F32)
-                gather_f32(c == 0 and t < 1, hop4[:], st[t], entries(n4_l, first, width))
-                nc.vector.tensor_tensor(y[:, t, :], st[t][:, cols], hop4[:], ALU.min)
-            nc.sync.dma_start(out_rows[:, :, cols], y[:])
-            y_grouped = sbuf(f"y_grouped{c}", [width, PACK], BF16)
-            y_words = sbuf(f"y_words{c}", [width], U32)
-            interleave(nc.vector.tensor_copy, y_grouped[:], y[:])
+
+        def fetch_st(c, t, first, width):
+            offsets = entries(n4_l, c * HALF + first, width)
+            gather_f32(False, hop4[c][t][:, first : first + width], st[t], offsets)
+
+        def smaller(c, t, first, width):
+            own = st[t][:, c * HALF + first : c * HALF + first + width]
+            nc.vector.tensor_tensor(y[c][:, t, first : first + width], own, hop4[c][t][:, first : first + width], ALU.min)
+
+        def quantize_y(c, first, width):
             nc.vector.quantize_mx(
-                out=y_words[:].bitcast(FP8X4),
-                scales=y_scales[:, cols],
-                in_=y_grouped[:].rearrange("p j t -> p (j t)"),
+                out=y_words[c][:, first : first + width].bitcast(FP8X4),
+                scales=y_scales[:, c * HALF + first : c * HALF + first + width],
+                in_=y_grouped[c][:, first : first + width, :].rearrange("p j t -> p (j t)"),
             )
-            nc.sync.dma_start(out_words[:, cols], y_words[:].bitcast(I32))
+
+        for t in range(PACK):
+            for c in range(2):
+                gather_f32(2 * t + c < N3_HALVES_ON_VECTOR, hop3[t][:, halves[c]], h2[t], entries(n3_l, c * HALF, HALF))
+        for t in range(PACK):
+            nc.vector.tensor_tensor(st[t][:], h2[t][:], hop3[t][:], ALU.max)
+        for t in range(PACK):
+            fetch_st(0, t, 0, HALF)
+        for t in range(last):
+            fetch_st(1, t, 0, HALF)
+        fetch_st(1, last, 0, QUARTER)
+        fetch_st(1, last, QUARTER, QUARTER)
+        for t in range(PACK):
+            smaller(0, t, 0, HALF)
+        nc.sync.dma_start(out_rows[:, :, halves[0]], y[0][:])
+        smaller(1, 0, 0, HALF)
+        interleave(nc.vector.tensor_copy, y_grouped[0][:], y[0][:])
+        smaller(1, 1, 0, HALF)
+        quantize_y(0, 0, HALF)
+        nc.sync.dma_start(out_words[:, halves[0]], y_words[0][:].bitcast(I32))
+        smaller(1, 2, 0, HALF)
+        smaller(1, last, 0, QUARTER)
+        smaller(1, last, QUARTER, QUARTER)
+        nc.sync.dma_start(out_rows[:, :, halves[1]], y[1][:])
+        interleave(nc.scalar.copy, y_grouped[1][:, :QUARTER, :], y[1][:, :, :QUARTER])
+        interleave(nc.vector.tensor_copy, y_grouped[1][:, QUARTER:, :], y[1][:, :, QUARTER:])
+        quantize_y(1, 0, QUARTER)
+        quantize_y(1, QUARTER, QUARTER)
+        nc.sync.dma_start(out_words[:, halves[1]], y_words[1][:].bitcast(I32))
         for q in range(4):
-            queue = nc.sync if q % 2 == 0 else nc.scalar
+            queue = nc.scalar if q % 2 == 0 else nc.sync
             queue.dma_start(out_2[0].bitcast(I32)[4 * q : 4 * q + 4, :], y_scales[:].bitcast(I32)[32 * q : 32 * q + 4, :])

@@ -78,13 +78,14 @@ def tile_picked_codefillhopmn_none_po_kernel(
 
         x_table_bytes = sbuf("x_table_bytes", [T], U8)
         d_table_bytes = sbuf("d_table_bytes", [G], U8)
-        zero_bytes(d_table_bytes)
+        nc.vector.memset(d_table_bytes[:].bitcast(I32)[:, : G // 8], 0)
+        nc.gpsimd.memset(d_table_bytes[:].bitcast(I32)[:, G // 8 :], 0)
         zero_bytes(x_table_bytes)
         k1_l = load_list("k1_l", k1)
         offs_l = load_list("offs_l", offs)
         n1_l = load_list("n1_l", n1)
-        n2_l = load_list("n2_l", n2)
         nc.sync.dma_start(d_table_bytes[:].bitcast(I32)[0:P:8, :], d_scales[0].bitcast(I32))
+        n2_l = load_list("n2_l", n2)
         nc.sync.dma_start(x_table_bytes[:].bitcast(I32)[0:P:8, :], x_scales[0].bitcast(I32))
         x_table_words = sbuf("x_table_words", [T], U32)
         d_table_words = sbuf("d_table_words", [G], U32)
@@ -133,25 +134,47 @@ def tile_picked_codefillhopmn_none_po_kernel(
         w2_picked = sbuf("w2_picked", [H], U32, tag="picked0")
         picked_bytes2 = sbuf("picked_bytes2", [H], U8, tag="picked1")
         dealt_bytes2 = sbuf("dealt_bytes2", [H], U8)
-        w2 = sbuf("w2", [PACK, P], U32)
         nc.vector.tensor_copy(w2_picked[:], d_table_words[:].indirect(k2_l[:]))
         nc.vector.tensor_copy(picked_bytes2[:], d_table_bytes[:].indirect(k2_l[:]))
-        deal_words(w2[:], w2_picked[:])
         deal_bytes(dealt_bytes2[:], picked_bytes2[:])
         place_scale_rows(scales2, dealt_bytes2, (nc.sync,))
 
         ds = [sbuf(f"ds{t}", [S], F32) for t in range(PACK)]
-        for group in ((0,), (1,), (2,), (3,)):
-            pa = sbuf(f"pa{group[0]}", [len(group) * W], F32)
-            pb = sbuf(f"pb{group[0]}", [len(group) * W], F32)
-            ra = sbuf(f"ra{group[0]}", [len(group) * W], F32)
-            for u, t in enumerate(group):
-                nc.scalar.activation(ds[t][:], banks1[t][:], COPY, scale=SIXTEENTH)
-                gather_f32(False, pa[:, u * W : (u + 1) * W], ds[t], n1_l[:])
-                gather_f32(False, pb[:, u * W : (u + 1) * W], ds[t], n2_l[:])
-            nc.vector.tensor_tensor(ra[:], pa[:], pb[:], ALU.max)
-            for u, t in enumerate(group):
-                nc.vector.tensor_copy(ds[t][:].indirect(n1_l[:]), ra[:, u * W : (u + 1) * W])
+        pa = [sbuf(f"pa{t}", [W], F32) for t in range(PACK)]
+        pb = [sbuf(f"pb{t}", [W], F32) for t in range(PACK)]
+        ra = [sbuf(f"ra{t}", [W], F32) for t in range(PACK)]
+
+        def leave_bank(t):
+            nc.scalar.activation(ds[t][:], banks1[t][:], COPY, scale=SIXTEENTH)
+
+        def fetch(dst, t, held, first, count):
+            gather_f32(False, dst[t][:, first : first + count], ds[t], entries(held, first, count))
+
+        def larger(t):
+            nc.vector.tensor_tensor(ra[t][:], pa[t][:], pb[t][:], ALU.max)
+
+        def put_back(t):
+            nc.vector.tensor_copy(ds[t][:].indirect(n1_l[:]), ra[t][:])
+
+        for t in range(2):
+            leave_bank(t)
+            fetch(pa, t, n1_l, 0, W)
+            fetch(pb, t, n2_l, 0, W)
+            larger(t)
+            put_back(t)
+        leave_bank(2)
+        leave_bank(3)
+        fetch(pa, 2, n1_l, 0, W)
+        fetch(pa, 3, n1_l, 0, W)
+        fetch(pb, 3, n2_l, 0, W // 2)
+        fetch(pb, 2, n2_l, 0, W)
+        fetch(pb, 3, n2_l, W // 2, W // 2)
+        larger(2)
+        larger(3)
+        put_back(2)
+        put_back(3)
+        w2 = sbuf("w2", [PACK, P], U32, tag="ra2")
+        deal_words(w2[:], w2_picked[:])
 
         z_rows = sbuf("z_rows", [PACK, S], BF16)
         z_grouped = sbuf("z_grouped", [S, PACK], BF16)

@@ -70,10 +70,10 @@ def tile_picked_codefillhopmn_none_po_kernel(
             for j in range(4):
                 queues[j % len(queues)].dma_start(dst[:].bitcast(I32)[j:P:32, :], src[:].bitcast(I32)[8 * j : P : 32, :])
 
-        def interleave(engine_copy, dst, src):
+        def interleave(engine_copy, dst, src, run=4):
             engine_copy(
-                dst.rearrange("p (c i) t -> p c t i", i=4),
-                src.rearrange("p t (c i) -> p c t i", i=4),
+                dst.rearrange("p (c i) t -> p c t i", i=run),
+                src.rearrange("p t (c i) -> p c t i", i=run),
             )
 
         x_table_bytes = sbuf("x_table_bytes", [T], U8)
@@ -92,8 +92,6 @@ def tile_picked_codefillhopmn_none_po_kernel(
         nc.sync.dma_start(x_table_words[:].bitcast(I32), x_words[0].rearrange("p n t -> p (n t)").bitcast(I32))
         nc.sync.dma_start(d_table_words[:].bitcast(I32), d_words[0].rearrange("p n t -> p (n t)").bitcast(I32))
         k2_l = load_list("k2_l", k2)
-        gs_t = sbuf("gs_t", [PACK], F32)
-        nc.sync.dma_start(gs_t[:], gs.rearrange("(p t) o -> p (t o)", t=PACK))
         n3_l = load_list("n3_l", n3)
         n4_l = load_list("n4_l", n4)
 
@@ -102,13 +100,15 @@ def tile_picked_codefillhopmn_none_po_kernel(
         zero_bytes(scales1)
         zero_bytes(scales2)
 
-        picked_bytes1 = sbuf("picked_bytes1", [S + H], U8)
+        picked_bytes1 = sbuf("picked_bytes1", [S + H], U8, tag="early")
         dealt_bytes1 = sbuf("dealt_bytes1", [S + H], U8)
         nc.vector.tensor_copy(picked_bytes1[:, S:], d_table_bytes[:].indirect(k1_l[:]))
         nc.vector.tensor_copy(picked_bytes1[:, :S], x_table_bytes[:].indirect(offs_l[:]))
         deal_bytes(dealt_bytes1[:, S:], picked_bytes1[:, S:])
         nc.vector.tensor_copy(dealt_bytes1[:].bitcast(I32)[:, : S // 4], picked_bytes1[:].bitcast(I32)[:, : S // 4])
-        place_scale_rows(scales1, dealt_bytes1, (nc.sync,))
+        place_scale_rows(scales1, dealt_bytes1, (nc.sync, nc.scalar))
+        gs_t = sbuf("gs_t", [PACK], F32, tag="early")
+        nc.sync.dma_start(gs_t[:], gs.rearrange("(p t) o -> p (t o)", t=PACK))
 
         x_picked = sbuf("x_picked", [S], U32)
         w1 = sbuf("w1", [PACK, P], U32)
@@ -119,14 +119,16 @@ def tile_picked_codefillhopmn_none_po_kernel(
         for u in range(2):
             deal_words(w1[:, :, u * P // 2 : (u + 1) * P // 2], w1_picked[u][:])
 
-        banks1 = [psum.tile([P, S], F32, name=f"bank1_{t}", tag=f"bank{t}") for t in range(PACK)]
-        for t in range(PACK):
+        halves = (slice(0, HALF), slice(HALF, S))
+        pieces = [(0, halves[0]), (0, halves[1])] + [(t, slice(0, S)) for t in range(1, PACK)]
+        banks1 = [psum.tile([P, S], F32, name=f"bank1_{u}", tag=f"bank{u}") for u in range(len(pieces))]
+        for u, (t, cols) in enumerate(pieces):
             nc.tensor.matmul_mx(
-                out=banks1[t][:],
+                out=banks1[u][:, cols],
                 lhsT=w1[:, t, :].bitcast(FP8X4),
                 lhsT_scale=scales1[:, S + t * P : S + (t + 1) * P],
-                rhs=x_picked[:].bitcast(FP8X4),
-                rhs_scale=scales1[:, :S],
+                rhs=x_picked[:, cols].bitcast(FP8X4),
+                rhs_scale=scales1[:, cols],
                 start=True,
                 stop=True,
             )
@@ -145,7 +147,9 @@ def tile_picked_codefillhopmn_none_po_kernel(
         ra = [sbuf(f"ra{t}", [W], F32) for t in range(PACK)]
 
         def leave_bank(t):
-            nc.scalar.activation(ds[t][:], banks1[t][:], COPY, scale=SIXTEENTH)
+            for u, (tile_no, cols) in enumerate(pieces):
+                if tile_no == t:
+                    nc.scalar.activation(ds[t][:, cols], banks1[u][:, cols], COPY, scale=SIXTEENTH)
 
         def fetch(dst, t, held, first, count):
             gather_f32(False, dst[t][:, first : first + count], ds[t], entries(held, first, count))
@@ -199,11 +203,9 @@ def tile_picked_codefillhopmn_none_po_kernel(
                 in_=z_grouped[:, cols, :].rearrange("p j t -> p (j t)"),
             )
 
-        halves = (slice(0, HALF), slice(HALF, S))
         h2 = [sbuf(f"h2_{t}", [S], F32) for t in range(PACK)]
-        pieces = [(0, halves[0]), (0, halves[1])] + [(t, slice(0, S)) for t in range(1, PACK)]
         for u, (t, cols) in enumerate(pieces):
-            bank = psum.tile([P, S], F32, name=f"bank2_{u}", tag=f"bank{(PACK + u) % 8}")
+            bank = psum.tile([P, S], F32, name=f"bank2_{u}", tag=f"bank{(len(pieces) + u) % 8}")
             nc.tensor.matmul_mx(
                 out=bank[:, cols],
                 lhsT=w2[:, t, :].bitcast(FP8X4),
@@ -255,7 +257,7 @@ def tile_picked_codefillhopmn_none_po_kernel(
             smaller(0, t, 0, HALF)
         nc.sync.dma_start(out_rows[:, :, halves[0]], y[0][:])
         smaller(1, 0, 0, HALF)
-        interleave(nc.vector.tensor_copy, y_grouped[0][:], y[0][:])
+        interleave(nc.vector.tensor_copy, y_grouped[0][:], y[0][:], 2)
         smaller(1, 1, 0, HALF)
         quantize_y(0, 0, HALF)
         nc.sync.dma_start(out_words[:, halves[0]], y_words[0][:].bitcast(I32))
@@ -263,8 +265,8 @@ def tile_picked_codefillhopmn_none_po_kernel(
         smaller(1, last, 0, QUARTER)
         smaller(1, last, QUARTER, QUARTER)
         nc.sync.dma_start(out_rows[:, :, halves[1]], y[1][:])
-        interleave(nc.scalar.copy, y_grouped[1][:, :QUARTER, :], y[1][:, :, :QUARTER])
-        interleave(nc.vector.tensor_copy, y_grouped[1][:, QUARTER:, :], y[1][:, :, QUARTER:])
+        interleave(nc.scalar.copy, y_grouped[1][:, :QUARTER, :], y[1][:, :, :QUARTER], 2)
+        interleave(nc.vector.tensor_copy, y_grouped[1][:, QUARTER:, :], y[1][:, :, QUARTER:], 2)
         quantize_y(1, 0, QUARTER)
         quantize_y(1, QUARTER, QUARTER)
         nc.sync.dma_start(out_words[:, halves[1]], y_words[1][:].bitcast(I32))

from contextlib import ExitStack

import concourse.mybir as mybir

K, T, S, G, H, W = 512, 1024, 512, 2048, 512, 256
FLOPS = 2 * 2 * K * H * S

F32 = mybir.dt.float32
BF16 = mybir.dt.bfloat16
I32 = mybir.dt.int32
U32 = mybir.dt.uint32
U16 = mybir.dt.uint16
U8 = mybir.dt.uint8
FP8X4 = mybir.dt.float8_e4m3fn_x4
COPY = mybir.ActivationFunctionType.Copy
ALU = mybir.AluOpType

P = 128
PACK = 4
SIXTEENTH = 0.0625
HALF = S // 2
Z_SPLIT = 320
QUARTER = S // 4
N3_HALVES_ON_VECTOR = 4


def tile_picked_codefillhopmn_none_po_kernel(
    tc, x_words, x_scales, d_words, d_scales, gs, offs, k1, n1, n2, k2, n3, n4, out_0, out_1, out_2
):
    nc = tc.nc

    with ExitStack() as ctx:
        lists = ctx.enter_context(tc.tile_pool(name="lists", bufs=1))
        sb = ctx.enter_context(tc.tile_pool(name="sb", bufs=1))
        psum = ctx.enter_context(tc.psum_pool(name="psum", bufs=1))

        def sbuf(name, width, dtype, tag=""):
            return sb.tile([P] + list(width), dtype, name=name, tag=tag or name, align_bytes=64)

        def load_list(name, src):
            held = lists.tile(list(src.shape), U16, name=name)
            nc.sync.dma_start(held[:], src)
            return held

        def entries(held, first, count):
            return held[:, first // 16 : (first + count) // 16]

        def zero_bytes(t):
            nc.vector.memset(t[:].bitcast(I32), 0)

        def gather_f32(on_vector, out, window, offsets):
            if on_vector:
                nc.vector.tensor_copy(out, window[:].indirect(offsets))
            else:
                nc.scalar.activation(out, window[:].indirect(offsets), COPY)

        def deal_words(dst, src):
            nc.vector.tensor_copy(
                dst.rearrange("p t (c i) -> p c t i", i=4),
                src.rearrange("p (c i t) -> p c t i", t=PACK, i=4),
            )

        def deal_bytes(dst, src):
            nc.vector.tensor_copy(
                dst.rearrange("p (t m) -> p t m", t=PACK),
                src.rearrange("p (m t) -> p t m", t=PACK),
            )

        def place_scale_rows(dst, src, queues):
            for j in range(4):
                queues[j % len(queues)].dma_start(dst[:].bitcast(I32)[j:P:32, :], src[:].bitcast(I32)[8 * j : P : 32, :])

        def interleave(engine_copy, dst, src, run=4):
            engine_copy(
                dst.rearrange("p (c i) t -> p c t i", i=run),
                src.rearrange("p t (c i) -> p c t i", i=run),
            )

        x_table_bytes = sbuf("x_table_bytes", [T], U8)
        d_table_bytes = sbuf("d_table_bytes", [G], U8)
        nc.vector.memset(d_table_bytes[:].bitcast(I32)[:, : G // 8], 0)
        nc.gpsimd.memset(d_table_bytes[:].bitcast(I32)[:, G // 8 :], 0)
        zero_bytes(x_table_bytes)
        k1_l = load_list("k1_l", k1)
        offs_l = load_list("offs_l", offs)
        n1_l = load_list("n1_l", n1)
        nc.sync.dma_start(d_table_bytes[:].bitcast(I32)[0:P:8, :], d_scales[0].bitcast(I32))
        n2_l = load_list("n2_l", n2)
        nc.sync.dma_start(x_table_bytes[:].bitcast(I32)[0:P:8, :], x_scales[0].bitcast(I32))
        x_table_words = sbuf("x_table_words", [T], U32)
        d_table_words = sbuf("d_table_words", [G], U32)
        nc.sync.dma_start(x_table_words[:].bitcast(I32), x_words[0].rearrange("p n t -> p (n t)").bitcast(I32))
        nc.sync.dma_start(d_table_words[:].bitcast(I32), d_words[0].rearrange("p n t -> p (n t)").bitcast(I32))
        k2_l = load_list("k2_l", k2)
        n3_l = load_list("n3_l", n3)
        n4_l = load_list("n4_l", n4)

        scales1 = sbuf("scales1", [S + H], U8)
        scales2 = sbuf("scales2", [H], U8)
        zero_bytes(scales1)
        zero_bytes(scales2)

        picked_bytes1 = sbuf("picked_bytes1", [S + H], U8, tag="early")
        dealt_bytes1 = sbuf("dealt_bytes1", [S + H], U8)
        nc.vector.tensor_copy(picked_bytes1[:, S:], d_table_bytes[:].indirect(k1_l[:]))
        nc.vector.tensor_copy(picked_bytes1[:, :S], x_table_bytes[:].indirect(offs_l[:]))
        deal_bytes(dealt_bytes1[:, S:], picked_bytes1[:, S:])
        nc.vector.tensor_copy(dealt_bytes1[:].bitcast(I32)[:, : S // 4], picked_bytes1[:].bitcast(I32)[:, : S // 4])
        place_scale_rows(scales1, dealt_bytes1, (nc.sync, nc.scalar))
        gs_t = sbuf("gs_t", [PACK], F32, tag="early")
        nc.sync.dma_start(gs_t[:], gs.rearrange("(p t) o -> p (t o)", t=PACK))

        x_picked = sbuf("x_picked", [S], U32)
        w1 = sbuf("w1", [PACK, P], U32)
        nc.vector.tensor_copy(x_picked[:], x_table_words[:].indirect(offs_l[:]))
        w1_picked = [sbuf(f"w1_picked{u}", [H // 2], U32, tag=f"picked{u}") for u in range(2)]
        for u in range(2):
            nc.vector.tensor_copy(w1_picked[u][:], d_table_words[:].indirect(entries(k1_l, u * H // 2, H // 2)))
        for u in range(2):
            deal_words(w1[:, :, u * P // 2 : (u + 1) * P // 2], w1_picked[u][:])

        halves = (slice(0, HALF), slice(HALF, S))
        pieces = [(0, halves[0]), (0, halves[1])] + [(t, slice(0, S)) for t in range(1, PACK)]
        banks1 = [psum.tile([P, S], F32, name=f"bank1_{u}", tag=f"bank{u}") for u in range(len(pieces))]
        for u, (t, cols) in enumerate(pieces):
            nc.tensor.matmul_mx(
                out=banks1[u][:, cols],
                lhsT=w1[:, t, :].bitcast(FP8X4),
                lhsT_scale=scales1[:, S + t * P : S + (t + 1) * P],
                rhs=x_picked[:, cols].bitcast(FP8X4),
                rhs_scale=scales1[:, cols],
                start=True,
                stop=True,
            )

        w2_picked = sbuf("w2_picked", [H], U32, tag="picked0")
        picked_bytes2 = sbuf("picked_bytes2", [H], U8, tag="picked1")
        dealt_bytes2 = sbuf("dealt_bytes2", [H], U8)
        nc.vector.tensor_copy(w2_picked[:], d_table_words[:].indirect(k2_l[:]))
        nc.vector.tensor_copy(picked_bytes2[:], d_table_bytes[:].indirect(k2_l[:]))
        deal_bytes(dealt_bytes2[:], picked_bytes2[:])
        place_scale_rows(scales2, dealt_bytes2, (nc.sync,))

        ds = [sbuf(f"ds{t}", [S], F32) for t in range(PACK)]
        pa = [sbuf(f"pa{t}", [W], F32) for t in range(PACK)]
        pb = [sbuf(f"pb{t}", [W], F32) for t in range(PACK)]
        ra = [sbuf(f"ra{t}", [W], F32) for t in range(PACK)]

        def leave_bank(t):
            for u, (tile_no, cols) in enumerate(pieces):
                if tile_no == t:
                    nc.scalar.activation(ds[t][:, cols], banks1[u][:, cols], COPY, scale=SIXTEENTH)

        def fetch(dst, t, held, first, count):
            gather_f32(False, dst[t][:, first : first + count], ds[t], entries(held, first, count))

        def larger(t):
            nc.vector.tensor_tensor(ra[t][:], pa[t][:], pb[t][:], ALU.max)

        def put_back(t):
            nc.vector.tensor_copy(ds[t][:].indirect(n1_l[:]), ra[t][:])

        for t in range(2):
            leave_bank(t)
            fetch(pa, t, n1_l, 0, W)
            fetch(pb, t, n2_l, 0, W)
            larger(t)
            put_back(t)
        leave_bank(2)
        leave_bank(3)
        fetch(pa, 2, n1_l, 0, W)
        fetch(pa, 3, n1_l, 0, W)
        fetch(pb, 3, n2_l, 0, W // 2)
        fetch(pb, 2, n2_l, 0, W)
        fetch(pb, 3, n2_l, W // 2, W // 2)
        larger(2)
        larger(3)
        put_back(2)
        put_back(3)
        w2 = sbuf("w2", [PACK, P], U32, tag="ra2")
        deal_words(w2[:], w2_picked[:])

        z_rows = sbuf("z_rows", [PACK, S], BF16)
        z_grouped = sbuf("z_grouped", [S, PACK], BF16)
        z_words = sbuf("z_words", [S], U32)
        z_scales = sbuf("z_scales", [S], U8)
        last = PACK - 1
        split = Z_SPLIT
        for t in range(last):
            nc.scalar.activation(z_rows[:, t, :], ds[t][:], COPY, scale=gs_t[:, t : t + 1])
        nc.scalar.activation(z_rows[:, last, split:], ds[last][:, split:], COPY, scale=gs_t[:, last : last + 1])
        interleave(nc.scalar.copy, z_grouped[:, split:, :], z_rows[:, :, split:])
        vector_cols = (slice(0, HALF), slice(HALF, split))
        for cols in vector_cols:
            nc.vector.tensor_scalar(z_rows[:, last, cols], ds[last][:, cols], gs_t[:, last : last + 1], None, ALU.mult)
        for cols in vector_cols:
            interleave(nc.vector.tensor_copy, z_grouped[:, cols, :], z_rows[:, :, cols])
        for c in range(2):
            cols = slice(c * HALF, (c + 1) * HALF)
            nc.vector.quantize_mx(
                out=z_words[:, cols].bitcast(FP8X4),
                scales=z_scales[:, cols],
                in_=z_grouped[:, cols, :].rearrange("p j t -> p (j t)"),
            )

        h2 = [sbuf(f"h2_{t}", [S], F32) for t in range(PACK)]
        for u, (t, cols) in enumerate(pieces):
            bank = psum.tile([P, S], F32, name=f"bank2_{u}", tag=f"bank{(len(pieces) + u) % 8}")
            nc.tensor.matmul_mx(
                out=bank[:, cols],
                lhsT=w2[:, t, :].bitcast(FP8X4),
                lhsT_scale=scales2[:, t * P : (t + 1) * P],
                rhs=z_words[:, cols].bitcast(FP8X4),
                rhs_scale=z_scales[:, cols],
                start=True,
                stop=True,
            )
            nc.scalar.activation(h2[t][:, cols], bank[:, cols], COPY, scale=SIXTEENTH)

        hop3 = [sbuf(f"hop3_{t}", [S], F32) for t in range(PACK)]
        st = [sbuf(f"st{t}", [S], F32) for t in range(PACK)]
        hop4 = [[sbuf(f"hop4_{c}_{t}", [HALF], F32) for t in range(PACK)] for c in range(2)]
        y = [sbuf(f"y{c}", [PACK, HALF], F32) for c in range(2)]
        y_grouped = [sbuf(f"y_grouped{c}", [HALF, PACK], BF16) for c in range(2)]
        y_words = [sbuf(f"y_words{c}", [HALF], U32) for c in range(2)]
        y_scales = sbuf("y_scales", [S], U8)
        out_rows = out_0.rearrange("(p t) j -> p t j", t=PACK)
        out_words = out_1[0].rearrange("p n t -> p (n t)").bitcast(I32)

        def fetch_st(c, t, first, width):
            offsets = entries(n4_l, c * HALF + first, width)
            gather_f32(False, hop4[c][t][:, first : first + width], st[t], offsets)

        def smaller(c, t, first, width):
            own = st[t][:, c * HALF + first : c * HALF + first + width]
            nc.vector.tensor_tensor(y[c][:, t, first : first + width], own, hop4[c][t][:, first : first + width], ALU.min)

        def quantize_y(c, first, width):
            nc.vector.quantize_mx(
                out=y_words[c][:, first : first + width].bitcast(FP8X4),
                scales=y_scales[:, c * HALF + first : c * HALF + first + width],
                in_=y_grouped[c][:, first : first + width, :].rearrange("p j t -> p (j t)"),
            )

        for t in range(PACK):
            for c in range(2):
                gather_f32(2 * t + c < N3_HALVES_ON_VECTOR, hop3[t][:, halves[c]], h2[t], entries(n3_l, c * HALF, HALF))
        for t in range(PACK):
            nc.vector.tensor_tensor(st[t][:], h2[t][:], hop3[t][:], ALU.max)
        for t in range(PACK):
            fetch_st(0, t, 0, HALF)
        for t in range(last):
            fetch_st(1, t, 0, HALF)
        fetch_st(1, last, 0, QUARTER)
        fetch_st(1, last, QUARTER, QUARTER)
        for t in range(PACK):
            smaller(0, t, 0, HALF)
        nc.sync.dma_start(out_rows[:, :, halves[0]], y[0][:])
        smaller(1, 0, 0, HALF)
        interleave(nc.vector.tensor_copy, y_grouped[0][:], y[0][:], 2)
        smaller(1, 1, 0, HALF)
        quantize_y(0, 0, HALF)
        nc.sync.dma_start(out_words[:, halves[0]], y_words[0][:].bitcast(I32))
        smaller(1, 2, 0, HALF)
        smaller(1, last, 0, QUARTER)
        smaller(1, last, QUARTER, QUARTER)
        nc.sync.dma_start(out_rows[:, :, halves[1]], y[1][:])
        interleave(nc.scalar.copy, y_grouped[1][:, :QUARTER, :], y[1][:, :, :QUARTER], 2)
        interleave(nc.vector.tensor_copy, y_grouped[1][:, QUARTER:, :], y[1][:, :, QUARTER:], 2)
        quantize_y(1, 0, QUARTER)
        quantize_y(1, QUARTER, QUARTER)
        nc.sync.dma_start(out_words[:, halves[1]], y_words[1][:].bitcast(I32))
        for q in range(4):
            queue = nc.scalar if q % 2 == 0 else nc.sync
            queue.dma_start(out_2[0].bitcast(I32)[4 * q : 4 * q + 4, :], y_scales[:].bitcast(I32)[32 * q : 32 * q + 4, :])
